import numpy as np
import ml_dtypes


def mxq(x, axis, fmt="e4m3"):
    dtype, down = {"e4m3": (ml_dtypes.float8_e4m3fn, 7), "e5m2": (ml_dtypes.float8_e5m2, 14)}[fmt]
    v = np.moveaxis(np.asarray(x, np.float32).astype(ml_dtypes.bfloat16).astype(np.float64), axis, -1)
    blocks = v.reshape(v.shape[:-1] + (-1, 32))
    amax = np.abs(blocks).max(-1, keepdims=True)
    byte = np.maximum(np.where(amax > 0, np.frexp(amax)[1] - 1 + 127, 0) - down, 1)
    scale = np.exp2(byte - 127.0)
    codes = (blocks / scale).astype(np.float32).astype(dtype).astype(np.float64)
    return np.moveaxis((codes * scale).reshape(v.shape), -1, axis)


WIDE = False


def mx_kscale(k):
    if not WIDE:
        return np.ones(k)
    levels = np.array([10, -10, 5, -5, 0])
    if k % 512:
        return np.exp2(np.random.permutation(np.resize(levels, k // 32))).repeat(32)
    a = np.empty((k // 512, 16))
    for p in range(k // 512):
        a[p, :8] = np.random.permutation(np.resize(levels, 8))
        for g in range(8):
            far = levels[np.abs(levels - a[p, g]) >= 10]
            a[p, g + 8] = far[np.random.randint(len(far))]
    return np.exp2(a.ravel()).repeat(32)


def f64(x):
    return np.asarray(x).astype(np.float64)


def striped8(idx):
    return np.concatenate([x.reshape(-1, 16).T for x in idx]).astype(np.uint16)


def runs(offs, k):
    lists = np.stack([offs[16 * r : 16 * r + 16].T.reshape(-1) for r in range(8)]).astype(np.int64)
    return lists[np.arange(k) % 512 // 64]


def pack_weight(w):
    k, n = w.shape
    w = f64(np.asarray(w, np.float32).astype(ml_dtypes.bfloat16)).reshape(k // 32, 32, n)
    amax = np.abs(w).max(1)
    byte = np.clip(np.where(amax > 0, np.frexp(amax)[1] - 1 + 127 - 7, 1), 1, 254)
    scaled = (w * np.exp2(127.0 - byte)[:, None, :]).reshape(k, n).astype(np.float32)
    words = np.ascontiguousarray(scaled.reshape(k // 512, 128, 4, n).transpose(0, 1, 3, 2)).astype(ml_dtypes.float8_e4m3fn).view(np.uint8)
    return words, np.ascontiguousarray(byte.astype(np.uint8).reshape(k // 512, 16, n))


def unpack_weight(words, scales):
    g, p, n, _ = words.shape
    vals = np.ascontiguousarray(words).view(ml_dtypes.float8_e4m3fn).astype(np.float64) * np.repeat(np.exp2(scales.astype(np.float64) - 127.0), 8, axis=1)[..., None]
    return vals.transpose(0, 1, 3, 2).reshape(g * 512, n)


K, T, S, H, G = 512, 2048, 512, 512, 2048


def setup_inputs():
    n = np.random.standard_normal
    s = mx_kscale(K)[:, None]
    packed_xT = pack_weight(n((K, T)) * s)
    packed_dT = pack_weight(n((K, G)) / s)
    return {
        "x_words": packed_xT[0],
        "x_scales": packed_xT[1],
        "w1": (n((K, H)) / np.sqrt(K) / s).astype(np.float32),
        "gs": (np.random.uniform(0.5, 1.5, (K, 1)) * s).astype(np.float32),
        "d_words": packed_dT[0],
        "d_scales": packed_dT[1],
        "offs": striped8(np.random.randint(0, T, (8, S))),
        "n1": striped8(np.stack([np.random.permutation(S) for _ in range(8)])),
        "n2": striped8(np.stack([np.random.permutation(S) for _ in range(8)])),
        "ka": striped8(np.random.randint(0, G, (8, H))),
        "kb": striped8(np.random.randint(0, G, (8, H))),
        "n3": striped8(np.stack([np.random.permutation(S) for _ in range(8)])),
        "n4": striped8(np.stack([np.random.permutation(S) for _ in range(8)])),
    }


def reference(x_words, x_scales, w1, gs, d_words, d_scales, offs, n1, n2, ka, kb, n3, n4):
    d_ka = unpack_weight(d_words, d_scales)[np.arange(K)[:, None], runs(ka, K)]
    xq = unpack_weight(x_words, x_scales)[np.arange(K)[:, None], runs(offs, K)]
    y = mxq(f64(w1), 0, "e4m3").T @ xq
    ds = np.zeros((H, S))
    ds[np.arange(H)[:, None], runs(n1, H)] = y
    z = f64(gs) * (np.maximum(y, ds[np.arange(H)[:, None], runs(n2, H)]))
    zq = mxq(z, 0, "e4m3")
    d_kb = unpack_weight(d_words, d_scales)[np.arange(K)[:, None], runs(kb, K)]
    h = 0.0625 * (d_ka.T @ zq + d_kb.T @ zq)
    ds2 = np.zeros((H, S))
    ds2[np.arange(H)[:, None], runs(n3, H)] = h
    ds3 = np.zeros((H, S))
    ds3[np.arange(H)[:, None], runs(n4, H)] = h
    return np.maximum(ds2, ds3)

@@ -1,0 +1,194 @@
+from contextlib import ExitStack
+
+import concourse.mybir as mybir
+
+K, T, S, H, G = 512, 2048, 512, 512, 2048
+FLOPS = 3 * 2 * 512 * 512 * 512
+
+F32 = mybir.dt.float32
+BF16 = mybir.dt.bfloat16
+I32 = mybir.dt.int32
+U32 = mybir.dt.uint32
+U16 = mybir.dt.uint16
+U8 = mybir.dt.uint8
+FP8X4 = mybir.dt.float8_e4m3fn_x4
+COPY = mybir.ActivationFunctionType.Copy
+MAX = mybir.AluOpType.max
+
+P = 128
+PACK = 4
+WIN = 1024
+HALF = 256
+
+
+def tile_picked_hdaqrelaysendtwo_none_p_kernel(tc, x_words, x_scales, w1, gs, d_words, d_scales, offs, n1, n2, ka, kb, n3, n4, out):
+    nc = tc.nc
+    halves = [slice(c * HALF, (c + 1) * HALF) for c in range(2)]
+    list_halves = [slice(c * HALF // 16, (c + 1) * HALF // 16) for c in range(2)]
+    with ExitStack() as ctx:
+        keep = ctx.enter_context(tc.tile_pool(name="keep", bufs=1))
+        psum = ctx.enter_context(tc.psum_pool(name="psum", bufs=1))
+
+        def load_list(name, src):
+            tile = keep.tile([P, S // 16], U16, name=name)
+            nc.sync.dma_start(tile[:], src)
+            return tile
+
+        def load_scale_table(name, src, clear, queue):
+            tile = keep.tile([P, T], U8, name=name)
+            words = tile[:].bitcast(I32)
+            clear.memset(words, 0)
+            for e in range(2):
+                queue.dma_start(words[e:P:16, :], src[0, e:16:2, :].bitcast(I32))
+            return tile
+
+        def load_word_table(name, src, tag):
+            tile = keep.tile([P, T], I32, name=name, tag=tag)
+            nc.sync.dma_start(tile[:], src[0].rearrange("p n t -> p (n t)").bitcast(I32))
+            return tile
+
+        def place_scale_rows(plane, picked, queue):
+            nc.vector.tensor_copy(plane.bitcast(I32), picked.bitcast(I32))
+            for e in range(2):
+                queue.dma_start(plane.bitcast(I32)[2 + e:P:32, :], picked.bitcast(I32)[16 + e:P:32, :])
+
+        offs_l = load_list("offs_l", offs)
+        xs_tab = load_scale_table("xs_tab", x_scales, nc.vector, nc.sync)
+        ds_tab = load_scale_table("ds_tab", d_scales, nc.gpsimd, nc.gpsimd)
+        ka_l = load_list("ka_l", ka)
+        w_raw = []
+        for c in range(2):
+            raw = keep.tile([P, PACK, HALF], F32, name=f"w_raw{c}")
+            nc.sync.dma_start(raw[:], w1.rearrange("(p j) c -> p j c", j=PACK)[:, :, halves[c]])
+            w_raw.append(raw)
+        xw_tab = load_word_table("xw_tab", x_words, "xw_tab")
+        kb_l = load_list("kb_l", kb)
+        n1_l = load_list("n1_l", n1)
+        n2_l = load_list("n2_l", n2)
+        gain = keep.tile([P, PACK], F32)
+        nc.gpsimd.dma_start(gain[:], gs.rearrange("(p t) o -> p (t o)", t=PACK))
+        n3_l = load_list("n3_l", n3)
+        n4_l = load_list("n4_l", n4)
+
+        x_bytes = keep.tile([P, S], U8, align_bytes=64)
+        nc.vector.tensor_copy(x_bytes[:], xs_tab[:].indirect(offs_l[:]))
+        x_plane = keep.tile([P, S], U8, align_bytes=64)
+        place_scale_rows(x_plane[:], x_bytes[:], nc.sync)
+
+        w_grouped = keep.tile([P, PACK, P, PACK], BF16, align_bytes=64)
+        for c in range(2):
+            nc.scalar.copy(w_grouped[:, :, c * P // 2:(c + 1) * P // 2, :].rearrange("p t m j -> p m j t"),
+                           w_raw[c][:].rearrange("p j (m t) -> p m j t", t=PACK))
+        w_codes = keep.tile([P, H], U32, align_bytes=64)
+        w_plane = keep.tile([P, H], U8, align_bytes=64)
+
+        x_codes = keep.tile([P, S], U32, align_bytes=64)
+        for c in range(2):
+            nc.vector.tensor_copy(x_codes[:, halves[c]], xw_tab[:].bitcast(U32).indirect(offs_l[:, list_halves[c]]))
+            if c == 0:
+                nc.vector.quantize_mx(w_codes[:].bitcast(FP8X4), w_plane[:], w_grouped[:].rearrange("p t m j -> p (t m j)"))
+
+        z_grouped = [keep.tile([P, HALF, PACK], BF16, align_bytes=64, name=f"z_grouped{c}") for c in range(2)]
+        y_banks, sent = {}, {}
+
+        y_tiles = {}
+
+        def project(t, parts):
+            y = keep.tile([P, S], F32, name=f"y{t}", tag=f"y{t}", align_bytes=64)
+            width = S // parts
+            for c in range(parts):
+                cols = slice(c * width, (c + 1) * width)
+                bank = psum.tile([P, width], F32, name=f"y_bank{t}_{c}", tag=f"bank{t + 4 * c}")
+                nc.tensor.matmul_mx(bank[:], lhsT=w_codes[:, t * P:(t + 1) * P].bitcast(FP8X4), lhsT_scale=w_plane[:, t * P:(t + 1) * P],
+                                    rhs=x_codes[:, cols].bitcast(FP8X4), rhs_scale=x_plane[:, cols], start=True, stop=True)
+                nc.scalar.copy(y[:, cols], bank[:])
+                y_banks[t, c] = bank
+            y_tiles[t] = y
+
+        def send(t, parts, ds_tag):
+            ds = keep.tile([P, WIN], F32, name=f"ds{t}", tag=ds_tag, align_bytes=64)
+            width = S // parts
+            for c in range(parts):
+                nc.vector.tensor_copy(ds[:].indirect(n1_l[:, c * width // 16:(c + 1) * width // 16]),
+                                      y_tiles[t][:, c * width:(c + 1) * width])
+            sent[t] = ds
+
+        def weigh(t, parts, bank_parts, larger_tag):
+            width = S // parts
+            for c in range(parts):
+                fetched = keep.tile([P, width], F32, name=f"fetched{t}_{c}", tag=f"fetched{t}_{c}", align_bytes=64)
+                nc.scalar.activation(fetched[:], sent[t][:].indirect(n2_l[:, c * width // 16:(c + 1) * width // 16]), COPY)
+                larger = keep.tile([P, width], F32, name=f"larger{t}_{c}", tag=larger_tag or f"larger{t}_{c}", align_bytes=64)
+                if bank_parts == 2:
+                    for b in range(2):
+                        nc.vector.tensor_tensor(larger[:, halves[b]], fetched[:, halves[b]], y_banks[t, b][:], MAX)
+                else:
+                    nc.vector.tensor_tensor(larger[:], fetched[:], y_banks[t, 0][:, c * width:(c + 1) * width], MAX)
+                for b in range(2):
+                    if parts == 1:
+                        nc.scalar.activation(z_grouped[b][:, :, t], larger[:, halves[b]], COPY, scale=gain[:, t:t + 1])
+                    elif b == c:
+                        nc.scalar.activation(z_grouped[b][:, :, t], larger[:], COPY, scale=gain[:, t:t + 1])
+
+        for t in range(PACK):
+            project(t, 2 if t == 0 else 1)
+        send(0, 2, "ds0")
+        d_bytes = keep.tile([P, 2, H], U8, align_bytes=64)
+        for a, lst in enumerate((ka_l, kb_l)):
+            nc.vector.tensor_copy(d_bytes[:, a, :], ds_tab[:].indirect(lst[:]))
+        d_dealt = keep.tile([P, 2, H], U8, align_bytes=64)
+        nc.vector.tensor_copy(d_dealt[:].rearrange("p a (t m) -> p a t m", t=PACK),
+                              d_bytes[:].rearrange("p a (m t) -> p a t m", t=PACK))
+        d_plane = keep.tile([P, 2 * H], U8, align_bytes=64)
+        place_scale_rows(d_plane[:], d_dealt[:].rearrange("p a m -> p (a m)"), nc.sync)
+        send(1, 1, "ds1")
+        send(2, 1, "ds2")
+        dw_tab = load_word_table("dw_tab", d_words, "xw_tab")
+        d_codes = keep.tile([P, 2, H], U32, align_bytes=64)
+
+        def pick_codewords(a, lst, tag):
+            picked = keep.tile([P, H], U32, name=f"d_picked{a}", tag=tag, align_bytes=64)
+            nc.vector.tensor_copy(picked[:], dw_tab[:].bitcast(U32).indirect(lst[:]))
+            nc.vector.tensor_copy(d_codes[:, a, :].rearrange("p (t m) -> p m t", t=PACK),
+                                  picked[:].rearrange("p (m t) -> p m t", t=PACK))
+
+        weigh(0, 1, 2, None)
+        weigh(1, 1, 1, "y2")
+        pick_codewords(0, ka_l, "fetched1_0")
+        weigh(2, 1, 1, None)
+        send(3, 1, "fetched2_0")
+        z_codes = keep.tile([P, S], U32, align_bytes=64)
+        z_plane = keep.tile([P, S], U8, align_bytes=64)
+        weigh(3, 2, 1, None)
+        pick_codewords(1, kb_l, "y3")
+        for c in range(2):
+            nc.vector.quantize_mx(z_codes[:, halves[c]].bitcast(FP8X4), z_plane[:, halves[c]],
+                                  z_grouped[c][:].rearrange("p s t -> p (s t)"))
+
+        def second_product(bank, t, cols):
+            for a in range(2):
+                nc.tensor.matmul_mx(bank, lhsT=d_codes[:, a, t * P:(t + 1) * P].bitcast(FP8X4),
+                                    lhsT_scale=d_plane[:, a * H + t * P:a * H + (t + 1) * P],
+                                    rhs=z_codes[:, cols].bitcast(FP8X4), rhs_scale=z_plane[:, cols],
+                                    start=(a == 0), stop=(a == 1))
+
+        out_rows = out.rearrange("(p t) s -> t p s", t=PACK)
+        for t in range(PACK):
+            h = keep.tile([P, S], F32, name=f"h{t}")
+            ds2 = keep.tile([P, WIN], F32, name=f"ds2_{t}")
+            if t == 0:
+                for c in range(2):
+                    bank = psum.tile([P, HALF], F32, name=f"h_bank0_{c}", tag=f"bank{5 + c}")
+                    second_product(bank[:], t, halves[c])
+                    nc.scalar.activation(h[:, halves[c]], bank[:], COPY, scale=0.0625)
+                    nc.vector.tensor_copy(ds2[:].indirect(n3_l[:, list_halves[c]]), h[:, halves[c]])
+            else:
+                bank = psum.tile([P, S], F32, name=f"h_bank{t}", tag=f"bank{(6 + t) % 8}")
+                second_product(bank[:], t, slice(0, S))
+                nc.scalar.activation(h[:], bank[:], COPY, scale=0.0625)
+                nc.vector.tensor_copy(ds2[:].indirect(n3_l[:]), h[:])
+            ds3 = keep.tile([P, WIN], F32, name=f"ds3_{t}")
+            nc.vector.tensor_copy(ds3[:].indirect(n4_l[:]), h[:])
+            result = keep.tile([P, S], F32, name=f"result{t}")
+            nc.vector.tensor_tensor(result[:], ds2[:, :S], ds3[:, :S], MAX)
+            nc.sync.dma_start(out_rows[t], result[:])

@@ -1,6 +1,7 @@
 from contextlib import ExitStack
 
 import concourse.mybir as mybir
+from concourse.masks import make_identity
 
 K, T, S, H, G = 512, 2048, 512, 512, 2048
 FLOPS = 3 * 2 * 512 * 512 * 512
@@ -13,6 +14,7 @@ U16 = mybir.dt.uint16
 U8 = mybir.dt.uint8
 FP8X4 = mybir.dt.float8_e4m3fn_x4
 COPY = mybir.ActivationFunctionType.Copy
+RELU = mybir.ActivationFunctionType.Relu
 MAX = mybir.AluOpType.max
 
 P = 128
@@ -24,7 +26,11 @@ HALF = 256
 def tile_picked_hdaqrelaysendtwo_none_p_kernel(tc, x_words, x_scales, w1, gs, d_words, d_scales, offs, n1, n2, ka, kb, n3, n4, out):
     nc = tc.nc
     halves = [slice(c * HALF, (c + 1) * HALF) for c in range(2)]
-    list_halves = [slice(c * HALF // 16, (c + 1) * HALF // 16) for c in range(2)]
+    whole = [slice(0, S)]
+
+    def entries(lst, cols):
+        return lst[:, cols.start // 16:cols.stop // 16]
+
     with ExitStack() as ctx:
         keep = ctx.enter_context(tc.tile_pool(name="keep", bufs=1))
         psum = ctx.enter_context(tc.psum_pool(name="psum", bufs=1))
@@ -34,34 +40,36 @@ def tile_picked_hdaqrelaysendtwo_none_p_kernel(tc, x_words, x_scales, w1, gs, d_
             nc.sync.dma_start(tile[:], src)
             return tile
 
-        def load_scale_table(name, src, clear, queue):
+        def load_scale_table(name, src, clear):
             tile = keep.tile([P, T], U8, name=name)
             words = tile[:].bitcast(I32)
             clear.memset(words, 0)
             for e in range(2):
-                queue.dma_start(words[e:P:16, :], src[0, e:16:2, :].bitcast(I32))
+                nc.sync.dma_start(words[e:P:16, :], src[0, e:16:2, :].bitcast(I32))
             return tile
 
-        def load_word_table(name, src, tag):
-            tile = keep.tile([P, T], I32, name=name, tag=tag)
+        def load_word_table(name, src):
+            tile = keep.tile([P, T], I32, name=name, tag="word_table")
             nc.sync.dma_start(tile[:], src[0].rearrange("p n t -> p (n t)").bitcast(I32))
             return tile
 
-        def place_scale_rows(plane, picked, queue):
+        def place_scale_rows(plane, picked):
             nc.vector.tensor_copy(plane.bitcast(I32), picked.bitcast(I32))
             for e in range(2):
-                queue.dma_start(plane.bitcast(I32)[2 + e:P:32, :], picked.bitcast(I32)[16 + e:P:32, :])
+                nc.sync.dma_start(plane.bitcast(I32)[2 + e:P:32, :], picked.bitcast(I32)[16 + e:P:32, :])
 
-        offs_l = load_list("offs_l", offs)
-        xs_tab = load_scale_table("xs_tab", x_scales, nc.vector, nc.sync)
-        ds_tab = load_scale_table("ds_tab", d_scales, nc.gpsimd, nc.gpsimd)
-        ka_l = load_list("ka_l", ka)
-        w_raw = []
-        for c in range(2):
+        def load_weight_half(c):
             raw = keep.tile([P, PACK, HALF], F32, name=f"w_raw{c}")
             nc.sync.dma_start(raw[:], w1.rearrange("(p j) c -> p j c", j=PACK)[:, :, halves[c]])
-            w_raw.append(raw)
-        xw_tab = load_word_table("xw_tab", x_words, "xw_tab")
+            return raw
+
+        offs_l = load_list("offs_l", offs)
+        w_raw = [load_weight_half(0)]
+        xs_tab = load_scale_table("xs_tab", x_scales, nc.vector)
+        w_raw.append(load_weight_half(1))
+        ds_tab = load_scale_table("ds_tab", d_scales, nc.gpsimd)
+        ka_l = load_list("ka_l", ka)
+        xw_tab = load_word_table("xw_tab", x_words)
         kb_l = load_list("kb_l", kb)
         n1_l = load_list("n1_l", n1)
         n2_l = load_list("n2_l", n2)
@@ -69,126 +77,143 @@ def tile_picked_hdaqrelaysendtwo_none_p_kernel(tc, x_words, x_scales, w1, gs, d_
         nc.gpsimd.dma_start(gain[:], gs.rearrange("(p t) o -> p (t o)", t=PACK))
         n3_l = load_list("n3_l", n3)
         n4_l = load_list("n4_l", n4)
+        identity = keep.tile([P, P], F32)
+        make_identity(nc, identity[:])
 
         x_bytes = keep.tile([P, S], U8, align_bytes=64)
         nc.vector.tensor_copy(x_bytes[:], xs_tab[:].indirect(offs_l[:]))
         x_plane = keep.tile([P, S], U8, align_bytes=64)
-        place_scale_rows(x_plane[:], x_bytes[:], nc.sync)
+        place_scale_rows(x_plane[:], x_bytes[:])
 
-        w_grouped = keep.tile([P, PACK, P, PACK], BF16, align_bytes=64)
+        w_grouped = keep.tile([P, PACK, P, PACK], BF16, align_bytes=64, tag="w_grouped")
         for c in range(2):
             nc.scalar.copy(w_grouped[:, :, c * P // 2:(c + 1) * P // 2, :].rearrange("p t m j -> p m j t"),
                            w_raw[c][:].rearrange("p j (m t) -> p m j t", t=PACK))
         w_codes = keep.tile([P, H], U32, align_bytes=64)
         w_plane = keep.tile([P, H], U8, align_bytes=64)
+        nc.vector.quantize_mx(w_codes[:].bitcast(FP8X4), w_plane[:], w_grouped[:].rearrange("p t m j -> p (t m j)"))
 
         x_codes = keep.tile([P, S], U32, align_bytes=64)
-        for c in range(2):
-            nc.vector.tensor_copy(x_codes[:, halves[c]], xw_tab[:].bitcast(U32).indirect(offs_l[:, list_halves[c]]))
-            if c == 0:
-                nc.vector.quantize_mx(w_codes[:].bitcast(FP8X4), w_plane[:], w_grouped[:].rearrange("p t m j -> p (t m j)"))
+        for cols in halves:
+            nc.vector.tensor_copy(x_codes[:, cols], xw_tab[:].bitcast(U32).indirect(entries(offs_l, cols)))
 
-        z_grouped = [keep.tile([P, HALF, PACK], BF16, align_bytes=64, name=f"z_grouped{c}") for c in range(2)]
-        y_banks, sent = {}, {}
-
-        y_tiles = {}
-
-        def project(t, parts):
+        y_banks, y_tiles, sent, fetched = {}, {}, {}, {}
+        for t in range(PACK):
+            rows = slice(t * P, (t + 1) * P)
             y = keep.tile([P, S], F32, name=f"y{t}", tag=f"y{t}", align_bytes=64)
-            width = S // parts
-            for c in range(parts):
-                cols = slice(c * width, (c + 1) * width)
-                bank = psum.tile([P, width], F32, name=f"y_bank{t}_{c}", tag=f"bank{t + 4 * c}")
-                nc.tensor.matmul_mx(bank[:], lhsT=w_codes[:, t * P:(t + 1) * P].bitcast(FP8X4), lhsT_scale=w_plane[:, t * P:(t + 1) * P],
+            for c, cols in enumerate(halves if t == 0 else whole):
+                bank = psum.tile([P, cols.stop - cols.start], F32, name=f"y_bank{t}_{c}", tag=f"bank{t + 4 * c}")
+                nc.tensor.matmul_mx(bank[:], lhsT=w_codes[:, rows].bitcast(FP8X4), lhsT_scale=w_plane[:, rows],
                                     rhs=x_codes[:, cols].bitcast(FP8X4), rhs_scale=x_plane[:, cols], start=True, stop=True)
                 nc.scalar.copy(y[:, cols], bank[:])
-                y_banks[t, c] = bank
+                y_banks[t] = bank
             y_tiles[t] = y
 
-        def send(t, parts, ds_tag):
-            ds = keep.tile([P, WIN], F32, name=f"ds{t}", tag=ds_tag, align_bytes=64)
-            width = S // parts
-            for c in range(parts):
-                nc.vector.tensor_copy(ds[:].indirect(n1_l[:, c * width // 16:(c + 1) * width // 16]),
-                                      y_tiles[t][:, c * width:(c + 1) * width])
+        da_bytes = keep.tile([P, H], U8, align_bytes=64)
+        nc.vector.tensor_copy(da_bytes[:], ds_tab[:].indirect(ka_l[:]))
+        db_bytes = keep.tile([P, H], U8, align_bytes=64, tag="w_grouped")
+        nc.vector.tensor_copy(db_bytes[:], ds_tab[:].indirect(kb_l[:]))
+        d_dealt = keep.tile([P, 2, H], U8, align_bytes=64)
+        for a, picked in enumerate((da_bytes, db_bytes)):
+            nc.vector.tensor_copy(d_dealt[:, a, :].rearrange("p (t m) -> p t m", t=PACK),
+                                  picked[:].rearrange("p (m t) -> p t m", t=PACK))
+        d_plane = keep.tile([P, 2 * H], U8, align_bytes=64)
+        place_scale_rows(d_plane[:], d_dealt[:].rearrange("p a m -> p (a m)"))
+        dw_tab = load_word_table("dw_tab", d_words)
+
+        z_grouped = [keep.tile([P, HALF, PACK], BF16, align_bytes=64, name=f"z_grouped{c}") for c in range(2)]
+        d_codes = keep.tile([P, 2, PACK, P], U32, align_bytes=64)
+
+        def send(t, tag):
+            ds = keep.tile([P, WIN], F32, name=f"ds{t}", tag=tag, align_bytes=64)
+            for cols in halves if t == 0 else whole:
+                nc.vector.tensor_copy(ds[:].indirect(entries(n1_l, cols)), y_tiles[t][:, cols])
             sent[t] = ds
 
-        def weigh(t, parts, bank_parts, larger_tag):
-            width = S // parts
-            for c in range(parts):
-                fetched = keep.tile([P, width], F32, name=f"fetched{t}_{c}", tag=f"fetched{t}_{c}", align_bytes=64)
-                nc.scalar.activation(fetched[:], sent[t][:].indirect(n2_l[:, c * width // 16:(c + 1) * width // 16]), COPY)
-                larger = keep.tile([P, width], F32, name=f"larger{t}_{c}", tag=larger_tag or f"larger{t}_{c}", align_bytes=64)
-                if bank_parts == 2:
-                    for b in range(2):
-                        nc.vector.tensor_tensor(larger[:, halves[b]], fetched[:, halves[b]], y_banks[t, b][:], MAX)
-                else:
-                    nc.vector.tensor_tensor(larger[:], fetched[:], y_banks[t, 0][:, c * width:(c + 1) * width], MAX)
-                for b in range(2):
-                    if parts == 1:
-                        nc.scalar.activation(z_grouped[b][:, :, t], larger[:, halves[b]], COPY, scale=gain[:, t:t + 1])
-                    elif b == c:
-                        nc.scalar.activation(z_grouped[b][:, :, t], larger[:], COPY, scale=gain[:, t:t + 1])
+        def fetch(t, cols):
+            tile = keep.tile([P, cols.stop - cols.start], F32, name=f"fetched{t}_{cols.start}", tag=f"fetched{t}_{cols.start}", align_bytes=64)
+            nc.scalar.activation(tile[:], sent[t][:].indirect(entries(n2_l, cols)), COPY)
+            fetched[t, cols.start] = tile
 
-        for t in range(PACK):
-            project(t, 2 if t == 0 else 1)
-        send(0, 2, "ds0")
-        d_bytes = keep.tile([P, 2, H], U8, align_bytes=64)
-        for a, lst in enumerate((ka_l, kb_l)):
-            nc.vector.tensor_copy(d_bytes[:, a, :], ds_tab[:].indirect(lst[:]))
-        d_dealt = keep.tile([P, 2, H], U8, align_bytes=64)
-        nc.vector.tensor_copy(d_dealt[:].rearrange("p a (t m) -> p a t m", t=PACK),
-                              d_bytes[:].rearrange("p a (m t) -> p a t m", t=PACK))
-        d_plane = keep.tile([P, 2 * H], U8, align_bytes=64)
-        place_scale_rows(d_plane[:], d_dealt[:].rearrange("p a m -> p (a m)"), nc.sync)
-        send(1, 1, "ds1")
-        send(2, 1, "ds2")
-        dw_tab = load_word_table("dw_tab", d_words, "xw_tab")
-        d_codes = keep.tile([P, 2, H], U32, align_bytes=64)
+        def weigh(t, cols, tag):
+            larger = keep.tile([P, cols.stop - cols.start], F32, name=f"larger{t}_{cols.start}", tag=tag, align_bytes=64)
+            nc.vector.tensor_tensor(larger[:], fetched[t, cols.start][:], (y_tiles[t] if t == 0 else y_banks[t])[:, cols], MAX)
+            for c in range(cols.start // HALF, cols.stop // HALF):
+                nc.scalar.activation(z_grouped[c][:, :, t], larger[:, c * HALF - cols.start:(c + 1) * HALF - cols.start], COPY,
+                                     scale=gain[:, t:t + 1])
 
-        def pick_codewords(a, lst, tag):
-            picked = keep.tile([P, H], U32, name=f"d_picked{a}", tag=tag, align_bytes=64)
-            nc.vector.tensor_copy(picked[:], dw_tab[:].bitcast(U32).indirect(lst[:]))
-            nc.vector.tensor_copy(d_codes[:, a, :].rearrange("p (t m) -> p m t", t=PACK),
+        def pick_codewords(a, lst, cols, tag):
+            picked = keep.tile([P, cols.stop - cols.start], U32, name=f"d_picked{a}_{cols.start}", tag=tag, align_bytes=64)
+            nc.vector.tensor_copy(picked[:], dw_tab[:].bitcast(U32).indirect(entries(lst, cols)))
+            return picked
+
+        def deal_codewords(a, cols, picked):
+            nc.vector.tensor_copy(d_codes[:, a, :, cols.start // PACK:cols.stop // PACK].rearrange("p t m -> p m t"),
                                   picked[:].rearrange("p (m t) -> p m t", t=PACK))
 
-        weigh(0, 1, 2, None)
-        weigh(1, 1, 1, "y2")
-        pick_codewords(0, ka_l, "fetched1_0")
-        weigh(2, 1, 1, None)
-        send(3, 1, "fetched2_0")
+        for t in range(PACK - 1):
+            send(t, f"ds{t}")
+        for t in range(PACK - 1):
+            fetch(t, whole[0])
+        weigh(0, whole[0], "larger0")
+        weigh(1, whole[0], "y2")
+        deal_codewords(0, whole[0], pick_codewords(0, ka_l, whole[0], "fetched1_0"))
+        weigh(2, whole[0], "larger2")
+        send(3, "fetched2_0")
+        for cols in halves:
+            fetch(3, cols)
+        first = pick_codewords(1, kb_l, halves[0], "y3")
+        weigh(3, halves[0], "larger3a")
+        second = pick_codewords(1, kb_l, halves[1], "fetched3_0")
+        weigh(3, halves[1], "larger3b")
+        deal_codewords(1, halves[0], first)
+        deal_codewords(1, halves[1], second)
         z_codes = keep.tile([P, S], U32, align_bytes=64)
         z_plane = keep.tile([P, S], U8, align_bytes=64)
-        weigh(3, 2, 1, None)
-        pick_codewords(1, kb_l, "y3")
-        for c in range(2):
-            nc.vector.quantize_mx(z_codes[:, halves[c]].bitcast(FP8X4), z_plane[:, halves[c]],
-                                  z_grouped[c][:].rearrange("p s t -> p (s t)"))
-
-        def second_product(bank, t, cols):
-            for a in range(2):
-                nc.tensor.matmul_mx(bank, lhsT=d_codes[:, a, t * P:(t + 1) * P].bitcast(FP8X4),
-                                    lhsT_scale=d_plane[:, a * H + t * P:a * H + (t + 1) * P],
-                                    rhs=z_codes[:, cols].bitcast(FP8X4), rhs_scale=z_plane[:, cols],
-                                    start=(a == 0), stop=(a == 1))
+        for c, cols in enumerate(halves):
+            nc.vector.quantize_mx(z_codes[:, cols].bitcast(FP8X4), z_plane[:, cols], z_grouped[c][:].rearrange("p s t -> p (s t)"))
 
         out_rows = out.rearrange("(p t) s -> t p s", t=PACK)
+        h_tiles = []
         for t in range(PACK):
             h = keep.tile([P, S], F32, name=f"h{t}")
+            for c, cols in enumerate(halves if t == 0 else whole):
+                bank = psum.tile([P, cols.stop - cols.start], F32, name=f"h_bank{t}_{c}", tag=f"bank{5 + c if t == 0 else (7, 0, 4)[t - 1]}")
+                for a in range(2):
+                    nc.tensor.matmul_mx(bank[:], lhsT=d_codes[:, a, t, :].bitcast(FP8X4),
+                                        lhsT_scale=d_plane[:, a * H + t * P:a * H + (t + 1) * P],
+                                        rhs=z_codes[:, cols].bitcast(FP8X4), rhs_scale=z_plane[:, cols],
+                                        start=(a == 0), stop=(a == 1))
+                nc.scalar.activation(h[:, cols], bank[:], COPY, scale=0.0625)
+            h_tiles.append(h)
+
+        def turned_sum(name, tag, terms):
+            bank = psum.tile([P, S], F32, name=name, tag=tag)
+            for b in range(S // P):
+                block = slice(b * P, (b + 1) * P)
+                for i, term in enumerate(terms):
+                    nc.tensor.matmul(bank[:, block], lhsT=term[:, block], rhs=identity[:], is_transpose=True,
+                                     start=(i == 0), stop=(i == len(terms) - 1))
+            return bank
+
+        for t in range(PACK):
             ds2 = keep.tile([P, WIN], F32, name=f"ds2_{t}")
-            if t == 0:
-                for c in range(2):
-                    bank = psum.tile([P, HALF], F32, name=f"h_bank0_{c}", tag=f"bank{5 + c}")
-                    second_product(bank[:], t, halves[c])
-                    nc.scalar.activation(h[:, halves[c]], bank[:], COPY, scale=0.0625)
-                    nc.vector.tensor_copy(ds2[:].indirect(n3_l[:, list_halves[c]]), h[:, halves[c]])
-            else:
-                bank = psum.tile([P, S], F32, name=f"h_bank{t}", tag=f"bank{(6 + t) % 8}")
-                second_product(bank[:], t, slice(0, S))
-                nc.scalar.activation(h[:], bank[:], COPY, scale=0.0625)
-                nc.vector.tensor_copy(ds2[:].indirect(n3_l[:]), h[:])
+            for cols in halves if t == 0 else whole:
+                nc.vector.tensor_copy(ds2[:].indirect(entries(n3_l, cols)), h_tiles[t][:, cols])
             ds3 = keep.tile([P, WIN], F32, name=f"ds3_{t}")
-            nc.vector.tensor_copy(ds3[:].indirect(n4_l[:]), h[:])
-            result = keep.tile([P, S], F32, name=f"result{t}")
-            nc.vector.tensor_tensor(result[:], ds2[:, :S], ds3[:, :S], MAX)
-            nc.sync.dma_start(out_rows[t], result[:])
+            nc.vector.tensor_copy(ds3[:].indirect(n4_l[:]), h_tiles[t][:])
+            if t < PACK - 1:
+                base_turned = keep.tile([P, S], F32, name=f"base_turned{t}")
+                nc.scalar.copy(base_turned[:], turned_sum(f"base_bank{t}", "bank1", [ds2])[:])
+                minus = keep.tile([P, S], F32, name=f"minus{t}")
+                nc.scalar.activation(minus[:], ds2[:, :S], COPY, scale=-1.0)
+                excess_turned = keep.tile([P, S], F32, name=f"excess_turned{t}")
+                nc.scalar.activation(excess_turned[:], turned_sum(f"excess_bank{t}", "bank2", [minus, ds3])[:], RELU)
+                result = keep.tile([P, S], F32, name=f"result{t}")
+                nc.scalar.copy(result[:], turned_sum(f"result_bank{t}", "bank3", [base_turned, excess_turned])[:])
+                nc.scalar.dma_start(out_rows[t], result[:])
+                continue
+            for c, cols in enumerate(halves if t == PACK - 1 else whole):
+                result = keep.tile([P, cols.stop - cols.start], F32, name=f"result{t}_{c}")
+                nc.vector.tensor_tensor(result[:], ds2[:, cols], ds3[:, cols], MAX)
+                nc.sync.dma_start(out_rows[t][:, cols], result[:])

@@ -25,8 +25,8 @@ HALF = 256
 
 def tile_picked_hdaqrelaysendtwo_none_p_kernel(tc, x_words, x_scales, w1, gs, d_words, d_scales, offs, n1, n2, ka, kb, n3, n4, out):
     nc = tc.nc
-    halves = [slice(c * HALF, (c + 1) * HALF) for c in range(2)]
-    whole = [slice(0, S)]
+    first, second, whole = slice(0, HALF), slice(HALF, S), slice(0, S)
+    halves = [first, second]
 
     def entries(lst, cols):
         return lst[:, cols.start // 16:cols.stop // 16]
@@ -44,24 +44,25 @@ def tile_picked_hdaqrelaysendtwo_none_p_kernel(tc, x_words, x_scales, w1, gs, d_
             tile = keep.tile([P, T], U8, name=name)
             words = tile[:].bitcast(I32)
             clear.memset(words, 0)
-            for e in range(2):
-                nc.sync.dma_start(words[e:P:16, :], src[0, e:16:2, :].bitcast(I32))
+            nc.sync.dma_start(words[0:P:8, :], src[0].bitcast(I32))
             return tile
 
-        def load_word_table(name, src):
-            tile = keep.tile([P, T], I32, name=name, tag="word_table")
+        def load_word_table(name, src, tag):
+            tile = keep.tile([P, T], I32, name=name, tag=tag, align_bytes=64)
             nc.sync.dma_start(tile[:], src[0].rearrange("p n t -> p (n t)").bitcast(I32))
             return tile
-
-        def place_scale_rows(plane, picked):
-            nc.vector.tensor_copy(plane.bitcast(I32), picked.bitcast(I32))
-            for e in range(2):
-                nc.sync.dma_start(plane.bitcast(I32)[2 + e:P:32, :], picked.bitcast(I32)[16 + e:P:32, :])
 
         def load_weight_half(c):
             raw = keep.tile([P, PACK, HALF], F32, name=f"w_raw{c}")
             nc.sync.dma_start(raw[:], w1.rearrange("(p j) c -> p j c", j=PACK)[:, :, halves[c]])
             return raw
+
+        def place_scale_rows(name, picked, width):
+            plane = keep.tile([P, width], U8, align_bytes=64, name=name)
+            nc.gpsimd.memset(plane[:].bitcast(I32), 0)
+            for i in range(4):
+                nc.sync.dma_start(plane[:].bitcast(I32)[i:P:32, :], picked.bitcast(I32)[8 * i:P:32, :])
+            return plane
 
         offs_l = load_list("offs_l", offs)
         w_raw = [load_weight_half(0)]
@@ -69,21 +70,22 @@ def tile_picked_hdaqrelaysendtwo_none_p_kernel(tc, x_words, x_scales, w1, gs, d_
         w_raw.append(load_weight_half(1))
         ds_tab = load_scale_table("ds_tab", d_scales, nc.gpsimd)
         ka_l = load_list("ka_l", ka)
-        xw_tab = load_word_table("xw_tab", x_words)
         kb_l = load_list("kb_l", kb)
         n1_l = load_list("n1_l", n1)
+        xw_tab = load_word_table("xw_tab", x_words, "xw_tab")
         n2_l = load_list("n2_l", n2)
-        gain = keep.tile([P, PACK], F32)
-        nc.gpsimd.dma_start(gain[:], gs.rearrange("(p t) o -> p (t o)", t=PACK))
         n3_l = load_list("n3_l", n3)
         n4_l = load_list("n4_l", n4)
-        identity = keep.tile([P, P], F32)
-        make_identity(nc, identity[:])
 
-        x_bytes = keep.tile([P, S], U8, align_bytes=64)
+        x_bytes = keep.tile([P, S], U8, align_bytes=64, tag="x_bytes")
         nc.vector.tensor_copy(x_bytes[:], xs_tab[:].indirect(offs_l[:]))
-        x_plane = keep.tile([P, S], U8, align_bytes=64)
-        place_scale_rows(x_plane[:], x_bytes[:])
+        x_plane = place_scale_rows("x_plane", x_bytes[:], S)
+        gain = keep.tile([P, PACK], F32, align_bytes=64, tag="x_bytes")
+        nc.sync.dma_start(gain[:], gs.rearrange("(p t) o -> p (t o)", t=PACK))
+
+        d_bytes = keep.tile([P, 2, H], U8, align_bytes=64)
+        for a, lst in enumerate((ka_l, kb_l)):
+            nc.vector.tensor_copy(d_bytes[:, a, :], ds_tab[:].indirect(lst[:]))
 
         w_grouped = keep.tile([P, PACK, P, PACK], BF16, align_bytes=64, tag="w_grouped")
         for c in range(2):
@@ -92,100 +94,79 @@ def tile_picked_hdaqrelaysendtwo_none_p_kernel(tc, x_words, x_scales, w1, gs, d_
         w_codes = keep.tile([P, H], U32, align_bytes=64)
         w_plane = keep.tile([P, H], U8, align_bytes=64)
         nc.vector.quantize_mx(w_codes[:].bitcast(FP8X4), w_plane[:], w_grouped[:].rearrange("p t m j -> p (t m j)"))
-
         x_codes = keep.tile([P, S], U32, align_bytes=64)
         for cols in halves:
             nc.vector.tensor_copy(x_codes[:, cols], xw_tab[:].bitcast(U32).indirect(entries(offs_l, cols)))
+        dw_tab = load_word_table("dw_tab", d_words, "w_grouped")
 
-        y_banks, y_tiles, sent, fetched = {}, {}, {}, {}
-        for t in range(PACK):
+        d_dealt = keep.tile([P, 2, H], U8, align_bytes=64, tag="xw_tab")
+        nc.vector.tensor_copy(d_dealt[:].rearrange("p a (t m) -> p a t m", t=PACK), d_bytes[:].rearrange("p a (m t) -> p a t m", t=PACK))
+        d_plane = place_scale_rows("d_plane", d_dealt[:].rearrange("p a m -> p (a m)"), 2 * H)
+        identity = keep.tile([P, P], F32)
+        make_identity(nc, identity[:])
+
+        pieces = [(0, first), (1, whole), (0, second), (2, whole), (3, whole)]
+        y_tiles = [keep.tile([P, S], F32, name=f"y{t}", tag=f"y{t}", align_bytes=64) for t in range(PACK)]
+        y_banks = {}
+        for i, (t, cols) in enumerate(pieces):
             rows = slice(t * P, (t + 1) * P)
-            y = keep.tile([P, S], F32, name=f"y{t}", tag=f"y{t}", align_bytes=64)
-            for c, cols in enumerate(halves if t == 0 else whole):
-                bank = psum.tile([P, cols.stop - cols.start], F32, name=f"y_bank{t}_{c}", tag=f"bank{t + 4 * c}")
-                nc.tensor.matmul_mx(bank[:], lhsT=w_codes[:, rows].bitcast(FP8X4), lhsT_scale=w_plane[:, rows],
-                                    rhs=x_codes[:, cols].bitcast(FP8X4), rhs_scale=x_plane[:, cols], start=True, stop=True)
-                nc.scalar.copy(y[:, cols], bank[:])
-                y_banks[t] = bank
-            y_tiles[t] = y
-
-        da_bytes = keep.tile([P, H], U8, align_bytes=64)
-        nc.vector.tensor_copy(da_bytes[:], ds_tab[:].indirect(ka_l[:]))
-        db_bytes = keep.tile([P, H], U8, align_bytes=64, tag="w_grouped")
-        nc.vector.tensor_copy(db_bytes[:], ds_tab[:].indirect(kb_l[:]))
-        d_dealt = keep.tile([P, 2, H], U8, align_bytes=64)
-        for a, picked in enumerate((da_bytes, db_bytes)):
-            nc.vector.tensor_copy(d_dealt[:, a, :].rearrange("p (t m) -> p t m", t=PACK),
-                                  picked[:].rearrange("p (m t) -> p t m", t=PACK))
-        d_plane = keep.tile([P, 2 * H], U8, align_bytes=64)
-        place_scale_rows(d_plane[:], d_dealt[:].rearrange("p a m -> p (a m)"))
-        dw_tab = load_word_table("dw_tab", d_words)
+            bank = psum.tile([P, cols.stop - cols.start], F32, name=f"y_bank{i}", tag=f"bank{i}")
+            nc.tensor.matmul_mx(bank[:], lhsT=w_codes[:, rows].bitcast(FP8X4), lhsT_scale=w_plane[:, rows],
+                                rhs=x_codes[:, cols].bitcast(FP8X4), rhs_scale=x_plane[:, cols], start=True, stop=True)
+            nc.scalar.copy(y_tiles[t][:, cols], bank[:])
+            y_banks[t] = bank
 
         z_grouped = [keep.tile([P, HALF, PACK], BF16, align_bytes=64, name=f"z_grouped{c}") for c in range(2)]
-        d_codes = keep.tile([P, 2, PACK, P], U32, align_bytes=64)
+        sent, fetched = {}, {}
 
-        def send(t, tag):
-            ds = keep.tile([P, WIN], F32, name=f"ds{t}", tag=tag, align_bytes=64)
-            for cols in halves if t == 0 else whole:
-                nc.vector.tensor_copy(ds[:].indirect(entries(n1_l, cols)), y_tiles[t][:, cols])
-            sent[t] = ds
+        def send(t, cols):
+            nc.vector.tensor_copy(sent[t][:].indirect(entries(n1_l, cols)), y_tiles[t][:, cols])
 
         def fetch(t, cols):
             tile = keep.tile([P, cols.stop - cols.start], F32, name=f"fetched{t}_{cols.start}", tag=f"fetched{t}_{cols.start}", align_bytes=64)
             nc.scalar.activation(tile[:], sent[t][:].indirect(entries(n2_l, cols)), COPY)
             fetched[t, cols.start] = tile
 
-        def weigh(t, cols, tag):
-            larger = keep.tile([P, cols.stop - cols.start], F32, name=f"larger{t}_{cols.start}", tag=tag, align_bytes=64)
+        def weigh(t, cols):
+            larger = keep.tile([P, cols.stop - cols.start], F32, name=f"larger{t}_{cols.start}")
             nc.vector.tensor_tensor(larger[:], fetched[t, cols.start][:], (y_tiles[t] if t == 0 else y_banks[t])[:, cols], MAX)
             for c in range(cols.start // HALF, cols.stop // HALF):
                 nc.scalar.activation(z_grouped[c][:, :, t], larger[:, c * HALF - cols.start:(c + 1) * HALF - cols.start], COPY,
                                      scale=gain[:, t:t + 1])
 
-        def pick_codewords(a, lst, cols, tag):
-            picked = keep.tile([P, cols.stop - cols.start], U32, name=f"d_picked{a}_{cols.start}", tag=tag, align_bytes=64)
-            nc.vector.tensor_copy(picked[:], dw_tab[:].bitcast(U32).indirect(entries(lst, cols)))
-            return picked
-
-        def deal_codewords(a, cols, picked):
-            nc.vector.tensor_copy(d_codes[:, a, :, cols.start // PACK:cols.stop // PACK].rearrange("p t m -> p m t"),
-                                  picked[:].rearrange("p (m t) -> p m t", t=PACK))
-
         for t in range(PACK - 1):
-            send(t, f"ds{t}")
-        for t in range(PACK - 1):
-            fetch(t, whole[0])
-        weigh(0, whole[0], "larger0")
-        weigh(1, whole[0], "y2")
-        deal_codewords(0, whole[0], pick_codewords(0, ka_l, whole[0], "fetched1_0"))
-        weigh(2, whole[0], "larger2")
-        send(3, "fetched2_0")
+            sent[t] = keep.tile([P, WIN], F32, name=f"ds{t}")
+        for t, cols in pieces[:-1]:
+            send(t, cols)
+        for t in (1, 0, 2):
+            fetch(t, whole)
+        for t in (1, 0, 2):
+            weigh(t, whole)
+        sent[3] = keep.tile([P, WIN], F32, name="ds3", tag="fetched2_0", align_bytes=64)
+        send(3, whole)
         for cols in halves:
             fetch(3, cols)
-        first = pick_codewords(1, kb_l, halves[0], "y3")
-        weigh(3, halves[0], "larger3a")
-        second = pick_codewords(1, kb_l, halves[1], "fetched3_0")
-        weigh(3, halves[1], "larger3b")
-        deal_codewords(1, halves[0], first)
-        deal_codewords(1, halves[1], second)
+        d_picked = keep.tile([P, 2, H], U32, tag="y3", align_bytes=64)
+        for a, lst in enumerate((ka_l, kb_l)):
+            nc.vector.tensor_copy(d_picked[:, a, :], dw_tab[:].bitcast(U32).indirect(lst[:]))
+            weigh(3, halves[a])
+        d_codes = keep.tile([P, 2, PACK, P], U32, align_bytes=64)
+        nc.vector.tensor_copy(d_codes[:].rearrange("p a t m -> p a m t"), d_picked[:].rearrange("p a (m t) -> p a m t", t=PACK))
         z_codes = keep.tile([P, S], U32, align_bytes=64)
         z_plane = keep.tile([P, S], U8, align_bytes=64)
         for c, cols in enumerate(halves):
             nc.vector.quantize_mx(z_codes[:, cols].bitcast(FP8X4), z_plane[:, cols], z_grouped[c][:].rearrange("p s t -> p (s t)"))
 
         out_rows = out.rearrange("(p t) s -> t p s", t=PACK)
-        h_tiles = []
-        for t in range(PACK):
-            h = keep.tile([P, S], F32, name=f"h{t}")
-            for c, cols in enumerate(halves if t == 0 else whole):
-                bank = psum.tile([P, cols.stop - cols.start], F32, name=f"h_bank{t}_{c}", tag=f"bank{5 + c if t == 0 else (7, 0, 4)[t - 1]}")
-                for a in range(2):
-                    nc.tensor.matmul_mx(bank[:], lhsT=d_codes[:, a, t, :].bitcast(FP8X4),
-                                        lhsT_scale=d_plane[:, a * H + t * P:a * H + (t + 1) * P],
-                                        rhs=z_codes[:, cols].bitcast(FP8X4), rhs_scale=z_plane[:, cols],
-                                        start=(a == 0), stop=(a == 1))
-                nc.scalar.activation(h[:, cols], bank[:], COPY, scale=0.0625)
-            h_tiles.append(h)
+        h_tiles = [keep.tile([P, S], F32, name=f"h{t}") for t in range(PACK)]
+        for i, (t, cols) in enumerate([(0, first), (0, second), (1, whole), (2, whole), (3, whole)]):
+            bank = psum.tile([P, cols.stop - cols.start], F32, name=f"h_bank{i}", tag=f"bank{(5 + i) % 8}")
+            for a in range(2):
+                nc.tensor.matmul_mx(bank[:], lhsT=d_codes[:, a, t, :].bitcast(FP8X4),
+                                    lhsT_scale=d_plane[:, a * H + t * P:a * H + (t + 1) * P],
+                                    rhs=z_codes[:, cols].bitcast(FP8X4), rhs_scale=z_plane[:, cols],
+                                    start=(a == 0), stop=(a == 1))
+            nc.scalar.activation(h_tiles[t][:, cols], bank[:], COPY, scale=0.0625)
 
         def turned_sum(name, tag, terms):
             bank = psum.tile([P, S], F32, name=name, tag=tag)
@@ -198,22 +179,22 @@ def tile_picked_hdaqrelaysendtwo_none_p_kernel(tc, x_words, x_scales, w1, gs, d_
 
         for t in range(PACK):
             ds2 = keep.tile([P, WIN], F32, name=f"ds2_{t}")
-            for cols in halves if t == 0 else whole:
-                nc.vector.tensor_copy(ds2[:].indirect(entries(n3_l, cols)), h_tiles[t][:, cols])
             ds3 = keep.tile([P, WIN], F32, name=f"ds3_{t}")
-            nc.vector.tensor_copy(ds3[:].indirect(n4_l[:]), h_tiles[t][:])
+            for cols in halves if t == 0 else [whole]:
+                nc.vector.tensor_copy(ds2[:].indirect(entries(n3_l, cols)), h_tiles[t][:, cols])
+                nc.vector.tensor_copy(ds3[:].indirect(entries(n4_l, cols)), h_tiles[t][:, cols])
             if t < PACK - 1:
                 base_turned = keep.tile([P, S], F32, name=f"base_turned{t}")
-                nc.scalar.copy(base_turned[:], turned_sum(f"base_bank{t}", "bank1", [ds2])[:])
+                nc.scalar.copy(base_turned[:], turned_sum(f"base_bank{t}", "bank2", [ds2])[:])
                 minus = keep.tile([P, S], F32, name=f"minus{t}")
                 nc.scalar.activation(minus[:], ds2[:, :S], COPY, scale=-1.0)
                 excess_turned = keep.tile([P, S], F32, name=f"excess_turned{t}")
-                nc.scalar.activation(excess_turned[:], turned_sum(f"excess_bank{t}", "bank2", [minus, ds3])[:], RELU)
+                nc.scalar.activation(excess_turned[:], turned_sum(f"excess_bank{t}", "bank3", [minus, ds3])[:], RELU)
                 result = keep.tile([P, S], F32, name=f"result{t}")
-                nc.scalar.copy(result[:], turned_sum(f"result_bank{t}", "bank3", [base_turned, excess_turned])[:])
+                nc.scalar.copy(result[:], turned_sum(f"result_bank{t}", "bank4", [base_turned, excess_turned])[:])
                 nc.scalar.dma_start(out_rows[t], result[:])
-                continue
-            for c, cols in enumerate(halves if t == PACK - 1 else whole):
-                result = keep.tile([P, cols.stop - cols.start], F32, name=f"result{t}_{c}")
-                nc.vector.tensor_tensor(result[:], ds2[:, cols], ds3[:, cols], MAX)
-                nc.sync.dma_start(out_rows[t][:, cols], result[:])
+            else:
+                for c, cols in enumerate(halves):
+                    result = keep.tile([P, HALF], F32, name=f"result{t}_{c}")
+                    nc.vector.tensor_tensor(result[:], ds2[:, cols], ds3[:, cols], MAX)
+                    nc.sync.dma_start(out_rows[t][:, cols], result[:])

from contextlib import ExitStack

import concourse.mybir as mybir
from concourse.masks import make_identity

K, T, S, H, G = 512, 2048, 512, 512, 2048
FLOPS = 3 * 2 * 512 * 512 * 512

F32 = mybir.dt.float32
BF16 = mybir.dt.bfloat16
I32 = mybir.dt.int32
U32 = mybir.dt.uint32
U16 = mybir.dt.uint16
U8 = mybir.dt.uint8
FP8X4 = mybir.dt.float8_e4m3fn_x4
COPY = mybir.ActivationFunctionType.Copy
RELU = mybir.ActivationFunctionType.Relu
MAX = mybir.AluOpType.max

P = 128
PACK = 4
WIN = 1024
HALF = 256


def tile_picked_hdaqrelaysendtwo_none_p_kernel(tc, x_words, x_scales, w1, gs, d_words, d_scales, offs, n1, n2, ka, kb, n3, n4, out):
    nc = tc.nc
    first, second, whole = slice(0, HALF), slice(HALF, S), slice(0, S)
    halves = [first, second]

    def entries(lst, cols):
        return lst[:, cols.start // 16:cols.stop // 16]

    with ExitStack() as ctx:
        keep = ctx.enter_context(tc.tile_pool(name="keep", bufs=1))
        psum = ctx.enter_context(tc.psum_pool(name="psum", bufs=1))

        def load_list(name, src):
            tile = keep.tile([P, S // 16], U16, name=name)
            nc.sync.dma_start(tile[:], src)
            return tile

        def load_scale_table(name, src, clear):
            tile = keep.tile([P, T], U8, name=name)
            words = tile[:].bitcast(I32)
            clear.memset(words, 0)
            nc.sync.dma_start(words[0:P:8, :], src[0].bitcast(I32))
            return tile

        def load_word_table(name, src, tag):
            tile = keep.tile([P, T], I32, name=name, tag=tag, align_bytes=64)
            nc.sync.dma_start(tile[:], src[0].rearrange("p n t -> p (n t)").bitcast(I32))
            return tile

        def load_weight_half(c):
            raw = keep.tile([P, PACK, HALF], F32, name=f"w_raw{c}")
            nc.sync.dma_start(raw[:], w1.rearrange("(p j) c -> p j c", j=PACK)[:, :, halves[c]])
            return raw

        def place_scale_rows(name, picked, width):
            plane = keep.tile([P, width], U8, align_bytes=64, name=name)
            nc.gpsimd.memset(plane[:].bitcast(I32), 0)
            for i in range(4):
                nc.sync.dma_start(plane[:].bitcast(I32)[i:P:32, :], picked.bitcast(I32)[8 * i:P:32, :])
            return plane

        offs_l = load_list("offs_l", offs)
        w_raw = [load_weight_half(0)]
        xs_tab = load_scale_table("xs_tab", x_scales, nc.vector)
        w_raw.append(load_weight_half(1))
        ds_tab = load_scale_table("ds_tab", d_scales, nc.gpsimd)
        ka_l = load_list("ka_l", ka)
        kb_l = load_list("kb_l", kb)
        n1_l = load_list("n1_l", n1)
        xw_tab = load_word_table("xw_tab", x_words, "xw_tab")
        n2_l = load_list("n2_l", n2)
        n3_l = load_list("n3_l", n3)
        n4_l = load_list("n4_l", n4)

        x_bytes = keep.tile([P, S], U8, align_bytes=64, tag="x_bytes")
        nc.vector.tensor_copy(x_bytes[:], xs_tab[:].indirect(offs_l[:]))
        x_plane = place_scale_rows("x_plane", x_bytes[:], S)
        gain = keep.tile([P, PACK], F32, align_bytes=64, tag="x_bytes")
        nc.sync.dma_start(gain[:], gs.rearrange("(p t) o -> p (t o)", t=PACK))

        d_bytes = keep.tile([P, 2, H], U8, align_bytes=64)
        for a, lst in enumerate((ka_l, kb_l)):
            nc.vector.tensor_copy(d_bytes[:, a, :], ds_tab[:].indirect(lst[:]))

        w_grouped = keep.tile([P, PACK, P, PACK], BF16, align_bytes=64, tag="w_grouped")
        for c in range(2):
            nc.scalar.copy(w_grouped[:, :, c * P // 2:(c + 1) * P // 2, :].rearrange("p t m j -> p m j t"),
                           w_raw[c][:].rearrange("p j (m t) -> p m j t", t=PACK))
        w_codes = keep.tile([P, H], U32, align_bytes=64)
        w_plane = keep.tile([P, H], U8, align_bytes=64)
        nc.vector.quantize_mx(w_codes[:].bitcast(FP8X4), w_plane[:], w_grouped[:].rearrange("p t m j -> p (t m j)"))
        x_codes = keep.tile([P, S], U32, align_bytes=64)
        for cols in halves:
            nc.vector.tensor_copy(x_codes[:, cols], xw_tab[:].bitcast(U32).indirect(entries(offs_l, cols)))
        dw_tab = load_word_table("dw_tab", d_words, "w_grouped")

        d_dealt = keep.tile([P, 2, H], U8, align_bytes=64, tag="xw_tab")
        nc.vector.tensor_copy(d_dealt[:].rearrange("p a (t m) -> p a t m", t=PACK), d_bytes[:].rearrange("p a (m t) -> p a t m", t=PACK))
        d_plane = place_scale_rows("d_plane", d_dealt[:].rearrange("p a m -> p (a m)"), 2 * H)
        identity = keep.tile([P, P], F32)
        make_identity(nc, identity[:])

        pieces = [(0, first), (1, whole), (0, second), (2, whole), (3, whole)]
        y_tiles = [keep.tile([P, S], F32, name=f"y{t}", tag=f"y{t}", align_bytes=64) for t in range(PACK)]
        y_banks = {}
        for i, (t, cols) in enumerate(pieces):
            rows = slice(t * P, (t + 1) * P)
            bank = psum.tile([P, cols.stop - cols.start], F32, name=f"y_bank{i}", tag=f"bank{i}")
            nc.tensor.matmul_mx(bank[:], lhsT=w_codes[:, rows].bitcast(FP8X4), lhsT_scale=w_plane[:, rows],
                                rhs=x_codes[:, cols].bitcast(FP8X4), rhs_scale=x_plane[:, cols], start=True, stop=True)
            nc.scalar.copy(y_tiles[t][:, cols], bank[:])
            y_banks[t] = bank

        z_grouped = [keep.tile([P, HALF, PACK], BF16, align_bytes=64, name=f"z_grouped{c}") for c in range(2)]
        sent, fetched = {}, {}

        def send(t, cols):
            nc.vector.tensor_copy(sent[t][:].indirect(entries(n1_l, cols)), y_tiles[t][:, cols])

        def fetch(t, cols):
            tile = keep.tile([P, cols.stop - cols.start], F32, name=f"fetched{t}_{cols.start}", tag=f"fetched{t}_{cols.start}", align_bytes=64)
            nc.scalar.activation(tile[:], sent[t][:].indirect(entries(n2_l, cols)), COPY)
            fetched[t, cols.start] = tile

        def weigh(t, cols):
            larger = keep.tile([P, cols.stop - cols.start], F32, name=f"larger{t}_{cols.start}")
            nc.vector.tensor_tensor(larger[:], fetched[t, cols.start][:], (y_tiles[t] if t == 0 else y_banks[t])[:, cols], MAX)
            for c in range(cols.start // HALF, cols.stop // HALF):
                nc.scalar.activation(z_grouped[c][:, :, t], larger[:, c * HALF - cols.start:(c + 1) * HALF - cols.start], COPY,
                                     scale=gain[:, t:t + 1])

        for t in range(PACK - 1):
            sent[t] = keep.tile([P, WIN], F32, name=f"ds{t}")
        for t, cols in pieces[:-1]:
            send(t, cols)
        for t in (1, 0, 2):
            fetch(t, whole)
        for t in (1, 0, 2):
            weigh(t, whole)
        sent[3] = keep.tile([P, WIN], F32, name="ds3", tag="fetched2_0", align_bytes=64)
        send(3, whole)
        for cols in halves:
            fetch(3, cols)
        d_picked = keep.tile([P, 2, H], U32, tag="y3", align_bytes=64)
        for a, lst in enumerate((ka_l, kb_l)):
            nc.vector.tensor_copy(d_picked[:, a, :], dw_tab[:].bitcast(U32).indirect(lst[:]))
            weigh(3, halves[a])
        d_codes = keep.tile([P, 2, PACK, P], U32, align_bytes=64)
        nc.vector.tensor_copy(d_codes[:].rearrange("p a t m -> p a m t"), d_picked[:].rearrange("p a (m t) -> p a m t", t=PACK))
        z_codes = keep.tile([P, S], U32, align_bytes=64)
        z_plane = keep.tile([P, S], U8, align_bytes=64)
        for c, cols in enumerate(halves):
            nc.vector.quantize_mx(z_codes[:, cols].bitcast(FP8X4), z_plane[:, cols], z_grouped[c][:].rearrange("p s t -> p (s t)"))

        out_rows = out.rearrange("(p t) s -> t p s", t=PACK)
        h_tiles = [keep.tile([P, S], F32, name=f"h{t}") for t in range(PACK)]
        for i, (t, cols) in enumerate([(0, first), (0, second), (1, whole), (2, whole), (3, whole)]):
            bank = psum.tile([P, cols.stop - cols.start], F32, name=f"h_bank{i}", tag=f"bank{(5 + i) % 8}")
            for a in range(2):
                nc.tensor.matmul_mx(bank[:], lhsT=d_codes[:, a, t, :].bitcast(FP8X4),
                                    lhsT_scale=d_plane[:, a * H + t * P:a * H + (t + 1) * P],
                                    rhs=z_codes[:, cols].bitcast(FP8X4), rhs_scale=z_plane[:, cols],
                                    start=(a == 0), stop=(a == 1))
            nc.scalar.activation(h_tiles[t][:, cols], bank[:], COPY, scale=0.0625)

        def turned_sum(name, tag, terms):
            bank = psum.tile([P, S], F32, name=name, tag=tag)
            for b in range(S // P):
                block = slice(b * P, (b + 1) * P)
                for i, term in enumerate(terms):
                    nc.tensor.matmul(bank[:, block], lhsT=term[:, block], rhs=identity[:], is_transpose=True,
                                     start=(i == 0), stop=(i == len(terms) - 1))
            return bank

        for t in range(PACK):
            ds2 = keep.tile([P, WIN], F32, name=f"ds2_{t}")
            ds3 = keep.tile([P, WIN], F32, name=f"ds3_{t}")
            for cols in halves if t == 0 else [whole]:
                nc.vector.tensor_copy(ds2[:].indirect(entries(n3_l, cols)), h_tiles[t][:, cols])
                nc.vector.tensor_copy(ds3[:].indirect(entries(n4_l, cols)), h_tiles[t][:, cols])
            if t < PACK - 1:
                base_turned = keep.tile([P, S], F32, name=f"base_turned{t}")
                nc.scalar.copy(base_turned[:], turned_sum(f"base_bank{t}", "bank2", [ds2])[:])
                minus = keep.tile([P, S], F32, name=f"minus{t}")
                nc.scalar.activation(minus[:], ds2[:, :S], COPY, scale=-1.0)
                excess_turned = keep.tile([P, S], F32, name=f"excess_turned{t}")
                nc.scalar.activation(excess_turned[:], turned_sum(f"excess_bank{t}", "bank3", [minus, ds3])[:], RELU)
                result = keep.tile([P, S], F32, name=f"result{t}")
                nc.scalar.copy(result[:], turned_sum(f"result_bank{t}", "bank4", [base_turned, excess_turned])[:])
                nc.scalar.dma_start(out_rows[t], result[:])
            else:
                for c, cols in enumerate(halves):
                    result = keep.tile([P, HALF], F32, name=f"result{t}_{c}")
                    nc.vector.tensor_tensor(result[:], ds2[:, cols], ds3[:, cols], MAX)
                    nc.sync.dma_start(out_rows[t][:, cols], result[:])
